import numpy as np
import ml_dtypes


def mxq(x, axis, fmt="e4m3"):
    dtype, down = {"e4m3": (ml_dtypes.float8_e4m3fn, 7), "e5m2": (ml_dtypes.float8_e5m2, 14)}[fmt]
    v = np.moveaxis(np.asarray(x, np.float32).astype(ml_dtypes.bfloat16).astype(np.float64), axis, -1)
    blocks = v.reshape(v.shape[:-1] + (-1, 32))
    amax = np.abs(blocks).max(-1, keepdims=True)
    byte = np.maximum(np.where(amax > 0, np.frexp(amax)[1] - 1 + 127, 0) - down, 1)
    scale = np.exp2(byte - 127.0)
    codes = (blocks / scale).astype(np.float32).astype(dtype).astype(np.float64)
    return np.moveaxis((codes * scale).reshape(v.shape), -1, axis)


WIDE = False


def mx_kscale(k, group=512):
    if not WIDE:
        return np.ones(k)
    levels = np.array([10, -10, 5, -5, 0])
    if group != 512:
        return np.exp2(np.random.permutation(np.resize(levels, k // group))).repeat(group)
    if k % 512:
        return np.exp2(np.random.permutation(np.resize(levels, k // 32))).repeat(32)
    a = np.empty((k // 512, 16))
    for p in range(k // 512):
        a[p, :8] = np.random.permutation(np.resize(levels, 8))
        for g in range(8):
            far = levels[np.abs(levels - a[p, g]) >= 10]
            a[p, g + 8] = far[np.random.randint(len(far))]
    return np.exp2(a.ravel()).repeat(32)


def f64(x):
    return np.asarray(x).astype(np.float64)


def striped(idx):
    return np.tile(np.asarray(idx).reshape(-1, 16).T, (8, 1)).astype(np.uint16)


def unstriped(offs):
    return offs[:16].T.reshape(-1).astype(np.int64)


H, KV, D, NQ, N = 4, 1, 256, 512, 512


def setup_inputs():
    n = np.random.standard_normal
    s = mx_kscale(D, 0)[:, None]
    u = mx_kscale(N)
    t = np.random.uniform(0.5, 2.0, N) * u
    v = n((KV, N, 128))
    return {
        "qT": (n((H, D, NQ)) * s * (0.70 / np.sqrt(D))).astype(np.float32),
        "kT": (n((KV, D, N)) / s).astype(np.float32),
        "t": t.reshape(N, 1).astype(np.float32),
        "v": (v / t[:, None]).astype(np.float32),
        "mask": (np.arange(N)[:, None] <= np.sort(np.random.randint(N // 4, N, NQ))[None, :]).astype(np.float32),
        "og": n((H, NQ, 128)).astype(np.float32),
    }


def reference(qT, kT, t, v, mask, og):
    a = np.repeat(mxq(f64(kT), 1, "e4m3"), H // KV, 0).transpose(0, 2, 1) @ mxq(f64(qT), 1, "e4m3")
    p = np.tanh(a)
    p = p * f64(mask)
    w = p * f64(t)
    y = mxq(w, 1, "e4m3").transpose(0, 2, 1) @ np.repeat(mxq(f64(v), 1, "e4m3"), H // KV, 0)
    y = y / 16.0
    y = y / (1.0 + np.exp(-f64(og)))
    return y

@@ -1,0 +1,249 @@
+from contextlib import ExitStack
+
+import concourse.mybir as mybir
+
+H, D, NQ, N, E = 4, 256, 512, 512, 128
+FLOPS = 2 * H * NQ * N * (D + E)
+
+F32 = mybir.dt.float32
+BF16 = mybir.dt.bfloat16
+U32 = mybir.dt.uint32
+U8 = mybir.dt.uint8
+FP8X4 = mybir.dt.float8_e4m3fn_x4
+ACT = mybir.ActivationFunctionType
+ALU = mybir.AluOpType
+
+P = 128
+PACK = 4
+ROWS = 64
+QC = 128
+CHUNKS = NQ // QC
+UNITS = CHUNKS * H
+PAIRS = UNITS // 2
+
+
+def tile_rows_a_tanh_mask_gate_kernel(tc, qT, kT, t, v, mask, og, out):
+    nc = tc.nc
+    with ExitStack() as ctx:
+        keep = ctx.enter_context(tc.tile_pool(name="keep", bufs=1))
+        psum = ctx.enter_context(tc.psum_pool(name="psum", bufs=1))
+        ctx.enter_context(tc.manual_schedule())
+
+        def sb(name, shape, dtype, tag=None, bufs=1):
+            return keep.tile(shape, dtype, name=name, tag=tag or name, bufs=bufs, align_bytes=64)
+
+        warm = sb("warm", [P, 8], F32)
+        nc.vector.memset(warm[:], 0.0)
+        warm_out = sb("warm_out", [P, 8], F32)
+
+        k_view = kT[0].rearrange("(p j) n -> p j n", j=PACK)
+        k_raw = [sb("k_raw%d" % a, [P, PACK, N // 2], F32) for a in range(2)]
+        for a in range(2):
+            cols = slice(a * (N // 2), (a + 1) * (N // 2))
+            nc.sync.dma_start(out=k_raw[a][0:ROWS], in_=k_view[:, :, cols])
+            nc.scalar.dma_start(out=k_raw[a][ROWS:P], in_=k_view[:, :, cols])
+        t_sb = sb("t_sb", [P, PACK], F32)
+        nc.scalar.dma_start(out=t_sb[:], in_=t.rearrange("(p r) o -> p (r o)", r=PACK))
+        nc.scalar.activation(out=warm_out[:], in_=warm[:], func=ACT.Sigmoid)
+
+        q_view = qT.rearrange("(g h) (p j) q -> g (h p) j q", h=2, j=PACK)
+        m_view = mask.rearrange("(p r) q -> p r q", r=PACK)
+        q_raw = {}
+        m_raw = {}
+        og_raw = {}
+
+        def load_q(pair, c0, c1):
+            tl = sb("q_raw%d_%d" % (pair, c0), [P, PACK, (c1 - c0) * QC], F32)
+            nc.sync.dma_start(out=tl[:], in_=q_view[pair][:, :, c0 * QC : c1 * QC])
+            for c in range(c0, c1):
+                q_raw[(c, pair)] = tl[:, :, (c - c0) * QC : (c - c0 + 1) * QC]
+
+        def load_m(c0, c1):
+            tl = sb("m_raw%d" % c0, [P, PACK, (c1 - c0) * QC], F32)
+            nc.sync.dma_start(out=tl[:], in_=m_view[:, :, c0 * QC : c1 * QC])
+            for c in range(c0, c1):
+                m_raw[c] = tl[:, :, (c - c0) * QC : (c - c0 + 1) * QC]
+
+        def load_og(c):
+            tl = sb("og_raw%d" % c, [P, H, E], F32)
+            nc.sync.dma_start(out=tl[:], in_=og[:, c * QC : (c + 1) * QC, :].rearrange("h q e -> q h e"))
+            og_raw[c] = tl
+
+        v_raw = sb("v_raw", [P, PACK, E], F32)
+        load_q(0, 0, 1)
+        load_m(0, 1)
+        load_q(1, 0, 1)
+        load_q(0, 1, 2)
+        load_m(1, 2)
+        nc.sync.dma_start(out=v_raw[:], in_=v[0].rearrange("(p r) e -> p r e", r=PACK))
+        load_q(1, 1, 2)
+        load_og(0)
+        load_q(0, 2, 4)
+        load_m(2, 4)
+        load_q(1, 2, 4)
+        for c in range(1, CHUNKS):
+            load_og(c)
+
+        def cast(engine, out_ap, in_ap):
+            if engine == "vector":
+                nc.vector.tensor_copy(out=out_ap, in_=in_ap)
+            else:
+                nc.scalar.copy(out=out_ap, in_=in_ap)
+
+        def quantize(name, grouped, width):
+            codes = sb(name + "_codes", [P, width], U32)
+            scales = sb(name + "_scales", [P, width], U8)
+            nc.vector.quantize_mx(out=codes[:].bitcast(FP8X4), scales=scales[:], in_=grouped)
+            return codes, scales
+
+        k_bf = sb("k_bf", [P, PACK, P, PACK], BF16)
+
+        def cast_k(engine, s0, s1):
+            a = s0 // ROWS
+            src = k_raw[a][:, :, (s0 - a * ROWS) * PACK : (s1 - a * ROWS) * PACK]
+            cast(engine, k_bf[:, :, s0:s1, :].rearrange("p r s j -> p s j r"),
+                 src.rearrange("p j (s r) -> p s j r", r=PACK))
+
+        q_bf = {}
+        q_mx = {}
+
+        def cast_q(engine, k):
+            c, pair = divmod(k, 2)
+            tl = sb("q_bf%d" % k, [P, QC * PACK], BF16, tag="q_bf", bufs=3)
+            cast(engine, tl[:].rearrange("p (c i j) -> p c j i", i=4, j=PACK),
+                 q_raw[(c, pair)].rearrange("p j (c i) -> p c j i", i=4))
+            q_bf[k] = tl
+
+        def quant_q(k):
+            q_mx[k] = quantize("q%d" % k, q_bf[k][:], QC)
+
+        mt = {}
+
+        def make_mt(c):
+            tl = sb("mt%d" % c, [P, QC // 4, PACK, 4], F32)
+            for r in range(PACK):
+                nc.vector.tensor_scalar(
+                    out=tl[:, :, r, :],
+                    in0=m_raw[c][:, r, :].rearrange("p (c i) -> p c i", i=4),
+                    scalar1=t_sb[:, r : r + 1], scalar2=None, op0=ALU.mult)
+            mt[c] = tl
+
+        score = {}
+
+        def scores(k):
+            banks = []
+            for g in range(2):
+                bank = psum.tile([P, PACK, QC], F32, name="score%d_%d" % (k, g), tag="score%d" % g, bufs=3)
+                banks.append(bank)
+                score[2 * k + g] = bank
+            q_codes, q_scales = q_mx[k]
+            for g in range(2):
+                rows = slice(g * ROWS, (g + 1) * ROWS)
+                for r in range(PACK):
+                    cols = slice(r * P, (r + 1) * P)
+                    nc.tensor.matmul_mx(
+                        out=banks[g][:, r, :],
+                        lhsT=k_mx[0][rows, cols].bitcast(FP8X4), lhsT_scale=k_mx[1][rows, cols],
+                        rhs=q_codes[rows, :].bitcast(FP8X4), rhs_scale=q_scales[rows, :],
+                        start=True, stop=True)
+
+        pt = {}
+
+        def tanh(u):
+            tl = sb("p%d" % u, [P, QC * PACK], F32, tag="p", bufs=4)
+            nc.scalar.activation(
+                out=tl[:].rearrange("p (c r i) -> p c r i", r=PACK, i=4),
+                in_=score[u][:].rearrange("p r (c i) -> p c r i", i=4), func=ACT.Tanh)
+            pt[u] = tl
+
+        w_bf = {}
+        w_mx = {}
+
+        def weigh(u):
+            tl = sb("w_bf%d" % u, [P, QC * PACK], BF16, tag="w_bf", bufs=3)
+            nc.vector.tensor_tensor(
+                out=tl[:].rearrange("p (c i r) -> p c r i", i=4, r=PACK),
+                in0=pt[u][:].rearrange("p (c r i) -> p c r i", r=PACK, i=4),
+                in1=mt[u // H][:], op=ALU.mult)
+            w_bf[u] = tl
+
+        def quant_w(u):
+            w_mx[u] = quantize("w%d" % u, w_bf[u][:], QC)
+
+        y = {}
+
+        def second(u):
+            c, h = divmod(u, H)
+            if h == 0:
+                y[c] = psum.tile([P, H, E], F32, name="y%d" % c, tag="y", bufs=2)
+            nc.tensor.matmul_mx(
+                out=y[c][:, h, :],
+                lhsT=w_mx[u][0][:].bitcast(FP8X4), lhsT_scale=w_mx[u][1][:],
+                rhs=v_mx[0][0][:].bitcast(FP8X4), rhs_scale=v_mx[0][1][:],
+                start=True, stop=True)
+
+        gate = {}
+
+        def sigmoid(c):
+            tl = sb("gate%d" % c, [P, H, E], F32)
+            nc.scalar.activation(out=tl[:], in_=og_raw[c][:], func=ACT.Sigmoid)
+            gate[c] = tl
+
+        def finish(c, h0, h1):
+            tl = sb("res%d_%d" % (c, h0), [P, h1 - h0, E], F32)
+            nc.vector.scalar_tensor_tensor(
+                out=tl[:], in0=y[c][:, h0:h1, :], scalar=1.0 / 16.0, in1=gate[c][:, h0:h1, :],
+                op0=ALU.mult, op1=ALU.mult)
+            nc.sync.dma_start(
+                out=out[h0:h1, c * QC : (c + 1) * QC, :].rearrange("h q e -> q h e"), in_=tl[:])
+
+        v_bf = sb("v_bf", [P, E * PACK], BF16)
+        v_mx = []
+
+        cast_k("vector", 0, 64)
+        cast_k("vector", 64, 104)
+        cast_k("scalar", 104, 128)
+        cast_q("scalar", 0)
+        k_mx = quantize("k", k_bf[:].rearrange("p r s j -> p (r s j)"), N)
+        quant_q(0)
+        scores(0)
+        make_mt(0)
+        cast_q("vector", 1)
+        tanh(0)
+        quant_q(1)
+        scores(1)
+
+        for u in range(UNITS):
+            k = u // 2
+            if u > 0:
+                tanh(u)
+            if u % 2 == 1 and k + 2 < PAIRS:
+                cast_q("scalar", k + 2)
+            if u == 2:
+                cast("scalar", v_bf[:].rearrange("p (c i r) -> p c r i", i=4, r=PACK),
+                     v_raw[:].rearrange("p r (c i) -> p c r i", i=4))
+            if u % H == 0 and u > 0:
+                sigmoid(u // H - 1)
+            if u == UNITS - 2:
+                sigmoid(CHUNKS - 1)
+            weigh(u)
+            if u % 2 == 0 and 2 <= k + 1 < PAIRS:
+                quant_q(k + 1)
+                scores(k + 1)
+            if u > 0:
+                quant_w(u - 1)
+            if u == 3:
+                v_mx.append(quantize("v", v_bf[:], E))
+                for uu in range(3):
+                    second(uu)
+            if u > 3:
+                second(u - 1)
+            if u % H == 3 and u + 1 < UNITS:
+                make_mt(u // H + 1)
+            if u % H == 1 and u > H:
+                finish(u // H - 1, 0, H)
+        finish(CHUNKS - 1, 0, 2)
+        quant_w(UNITS - 1)
+        second(UNITS - 1)
+        finish(CHUNKS - 1, 2, 3)
+        finish(CHUNKS - 1, 3, 4)

@@ -20,6 +20,9 @@ QC = 128
 CHUNKS = NQ // QC
 UNITS = CHUNKS * H
 PAIRS = UNITS // 2
+ORDER = [(0, 0), (0, 1), (1, 0), (1, 1), (2, 0), (2, 1), (3, 0), (3, 1)]
+LOADS = [("q", 0, 0, 1), ("q", 1, 0, 1), ("m", 0, 1), ("q", 0, 1, 2), ("q", 1, 1, 2), ("v",), ("m", 1, 2), ("q", 0, 2, 4), ("q", 1, 2, 4), ("og", 1), ("m", 2, 4), ("og", 0), ("og", 3), ("og", 2)]
+SCHEDULE = [("CK", "scalar", 104, 128), ("CK", "vector", 0, 64), ("CK", "vector", 64, 104), ("C", "scalar", 0), ("QK",), ("QQ", 0), ("S", 0), ("C", "scalar", 1), ("QQ", 1), ("M", 0), ("C", "vector", 2), ("S", 1), ("T", 0), ("T", 1), ("W", 0, 0, 1), ("QQ", 2), ("S", 2), ("W", 0, 1, 2), ("T", 2), ("C", "scalar", 3), ("T", 3), ("CV", "scalar"), ("QW", 0, 0, 2), ("QQ", 3), ("T", 4), ("S", 3), ("M", 1), ("W", 1, 0, 2), ("T", 5), ("QV",), ("QW", 1, 0, 2), ("C", "scalar", 6), ("W", 2, 0, 1), ("C", "scalar", 4), ("T", 6), ("T", 7), ("W", 2, 1, 2), ("QQ", 4), ("QQ", 6), ("W", 3, 0, 1), ("S", 4), ("PV", 0), ("PV", 3), ("C", "scalar", 5), ("W", 3, 1, 2), ("PV", 1), ("T", 8), ("G", 1), ("S", 6), ("PV", 2), ("T", 9), ("QW", 2, 0, 2), ("M", 2), ("M", 3), ("PV", 4), ("QQ", 5), ("T", 12), ("QW", 3, 0, 2), ("PV", 5), ("S", 5), ("PV", 7), ("W", 4, 0, 2), ("PV", 6), ("G", 0), ("T", 10), ("T", 11), ("F", 0, 0, 4), ("C", "scalar", 7), ("T", 13), ("QW", 4, 0, 2), ("W", 5, 0, 1), ("W", 5, 1, 2), ("QQ", 7), ("W", 6, 0, 2), ("S", 7), ("PV", 8), ("T", 14), ("PV", 9), ("QW", 5, 0, 2), ("G", 2), ("T", 15), ("QW", 6, 0, 2), ("F", 1, 0, 4), ("W", 7, 0, 1), ("PV", 11), ("PV", 10), ("F", 2, 0, 4), ("PV", 12), ("W", 7, 1, 2), ("QW", 7, 0, 1), ("PV", 13), ("PV", 14), ("QW", 7, 1, 2), ("G", 3), ("F", 3, 0, 2), ("PV", 15), ("F", 3, 2, 4)]
 
 
 def tile_rows_a_tanh_mask_gate_kernel(tc, qT, kT, t, v, mask, og, out):
@@ -70,19 +73,13 @@ def tile_rows_a_tanh_mask_gate_kernel(tc, qT, kT, t, v, mask, og, out):
             og_raw[c] = tl
 
         v_raw = sb("v_raw", [P, PACK, E], F32)
-        load_q(0, 0, 1)
-        load_m(0, 1)
-        load_q(1, 0, 1)
-        load_q(0, 1, 2)
-        load_m(1, 2)
-        nc.sync.dma_start(out=v_raw[:], in_=v[0].rearrange("(p r) e -> p r e", r=PACK))
-        load_q(1, 1, 2)
-        load_og(0)
-        load_q(0, 2, 4)
-        load_m(2, 4)
-        load_q(1, 2, 4)
-        for c in range(1, CHUNKS):
-            load_og(c)
+
+        def load_v():
+            nc.sync.dma_start(out=v_raw[:], in_=v[0].rearrange("(p r) e -> p r e", r=PACK))
+
+        loads = {"q": load_q, "m": load_m, "og": load_og, "v": load_v}
+        for step in LOADS:
+            loads[step[0]](*step[1:])
 
         def cast(engine, out_ap, in_ap):
             if engine == "vector":
@@ -101,17 +98,17 @@ def tile_rows_a_tanh_mask_gate_kernel(tc, qT, kT, t, v, mask, og, out):
         def cast_k(engine, s0, s1):
             a = s0 // ROWS
             src = k_raw[a][:, :, (s0 - a * ROWS) * PACK : (s1 - a * ROWS) * PACK]
-            cast(engine, k_bf[:, :, s0:s1, :].rearrange("p r s j -> p s j r"),
-                 src.rearrange("p j (s r) -> p s j r", r=PACK))
+            cast(engine, k_bf[:, :, s0:s1, :].rearrange("p (a b) s j -> p a s j b", b=2),
+                 src.rearrange("p j (s a b) -> p a s j b", a=2, b=2))
 
         q_bf = {}
         q_mx = {}
 
         def cast_q(engine, k):
-            c, pair = divmod(k, 2)
-            tl = sb("q_bf%d" % k, [P, QC * PACK], BF16, tag="q_bf", bufs=3)
-            cast(engine, tl[:].rearrange("p (c i j) -> p c j i", i=4, j=PACK),
-                 q_raw[(c, pair)].rearrange("p j (c i) -> p c j i", i=4))
+            c, pair = ORDER[k]
+            tl = sb("q_bf%d" % k, [P, QC * PACK], BF16, tag="q_bf", bufs=4)
+            cast(engine, tl[:].rearrange("p (c i j) -> p c j i", i=2, j=PACK),
+                 q_raw[(c, pair)].rearrange("p j (c i) -> p c j i", i=2))
             q_bf[k] = tl
 
         def quant_q(k):
@@ -120,12 +117,12 @@ def tile_rows_a_tanh_mask_gate_kernel(tc, qT, kT, t, v, mask, og, out):
         mt = {}
 
         def make_mt(c):
-            tl = sb("mt%d" % c, [P, QC // 4, PACK, 4], F32)
-            for r in range(PACK):
-                nc.vector.tensor_scalar(
-                    out=tl[:, :, r, :],
-                    in0=m_raw[c][:, r, :].rearrange("p (c i) -> p c i", i=4),
-                    scalar1=t_sb[:, r : r + 1], scalar2=None, op0=ALU.mult)
+            tl = sb("mt%d" % c, [P, QC * PACK], F32)
+            nc.vector.tensor_tensor(
+                out=tl[:].rearrange("p (c i r) -> p c r i", i=2, r=PACK),
+                in0=m_raw[c].rearrange("p r (c i) -> p c r i", i=2),
+                in1=t_sb[:].unsqueeze(1).unsqueeze(3).to_broadcast([P, QC // 2, PACK, 2]),
+                op=ALU.mult)
             mt[c] = tl
 
         score = {}
@@ -150,35 +147,40 @@ def tile_rows_a_tanh_mask_gate_kernel(tc, qT, kT, t, v, mask, og, out):
         pt = {}
 
         def tanh(u):
-            tl = sb("p%d" % u, [P, QC * PACK], F32, tag="p", bufs=4)
+            k, g = divmod(u, 2)
+            if g == 0:
+                pt[k] = sb("p%d" % k, [P, 2, QC * PACK], F32, tag="p", bufs=4)
             nc.scalar.activation(
-                out=tl[:].rearrange("p (c r i) -> p c r i", r=PACK, i=4),
-                in_=score[u][:].rearrange("p r (c i) -> p c r i", i=4), func=ACT.Tanh)
-            pt[u] = tl
+                out=pt[k][:, g, :].rearrange("p (q r) -> p q r", r=PACK),
+                in_=score[u][:].rearrange("p r q -> p q r"), func=ACT.Tanh)
 
         w_bf = {}
         w_mx = {}
 
-        def weigh(u):
-            tl = sb("w_bf%d" % u, [P, QC * PACK], BF16, tag="w_bf", bufs=3)
+        def weigh(k, g0, g1):
+            if g0 == 0:
+                w_bf[k] = sb("w_bf%d" % k, [P, 2, QC * PACK], BF16, tag="w_bf", bufs=4)
             nc.vector.tensor_tensor(
-                out=tl[:].rearrange("p (c i r) -> p c r i", i=4, r=PACK),
-                in0=pt[u][:].rearrange("p (c r i) -> p c r i", r=PACK, i=4),
-                in1=mt[u // H][:], op=ALU.mult)
-            w_bf[u] = tl
+                out=w_bf[k][:, g0:g1, :], in0=pt[k][:, g0:g1, :],
+                in1=mt[ORDER[k][0]][:].unsqueeze(1).to_broadcast([P, g1 - g0, QC * PACK]), op=ALU.mult)
 
-        def quant_w(u):
-            w_mx[u] = quantize("w%d" % u, w_bf[u][:], QC)
+        def quant_w(k, g0, g1):
+            codes, scales = quantize("w%d_%d" % (k, g0), w_bf[k][:, g0:g1, :].rearrange("p g x -> p (g x)"), (g1 - g0) * QC)
+            for g in range(g0, g1):
+                cols = slice((g - g0) * QC, (g - g0 + 1) * QC)
+                w_mx[2 * k + g] = (codes[:, cols], scales[:, cols])
 
         y = {}
 
         def second(u):
-            c, h = divmod(u, H)
-            if h == 0:
-                y[c] = psum.tile([P, H, E], F32, name="y%d" % c, tag="y", bufs=2)
+            c, h = ORDER[u // 2][0], 2 * ORDER[u // 2][1] + u % 2
+            if h == 0 or u == UNITS - 2:
+                bank = psum.tile([P, H, E], F32, name="y%d" % u, tag="y", bufs=2)
+                for hh in range(h, H):
+                    y[(c, hh)] = bank
             nc.tensor.matmul_mx(
-                out=y[c][:, h, :],
-                lhsT=w_mx[u][0][:].bitcast(FP8X4), lhsT_scale=w_mx[u][1][:],
+                out=y[(c, h)][:, h, :],
+                lhsT=w_mx[u][0].bitcast(FP8X4), lhsT_scale=w_mx[u][1],
                 rhs=v_mx[0][0][:].bitcast(FP8X4), rhs_scale=v_mx[0][1][:],
                 start=True, stop=True)
 
@@ -192,7 +194,7 @@ def tile_rows_a_tanh_mask_gate_kernel(tc, qT, kT, t, v, mask, og, out):
         def finish(c, h0, h1):
             tl = sb("res%d_%d" % (c, h0), [P, h1 - h0, E], F32)
             nc.vector.scalar_tensor_tensor(
-                out=tl[:], in0=y[c][:, h0:h1, :], scalar=1.0 / 16.0, in1=gate[c][:, h0:h1, :],
+                out=tl[:], in0=y[(c, h0)][:, h0:h1, :], scalar=1.0 / 16.0, in1=gate[c][:, h0:h1, :],
                 op0=ALU.mult, op1=ALU.mult)
             nc.sync.dma_start(
                 out=out[h0:h1, c * QC : (c + 1) * QC, :].rearrange("h q e -> q h e"), in_=tl[:])
@@ -200,50 +202,25 @@ def tile_rows_a_tanh_mask_gate_kernel(tc, qT, kT, t, v, mask, og, out):
         v_bf = sb("v_bf", [P, E * PACK], BF16)
         v_mx = []
 
-        cast_k("vector", 0, 64)
-        cast_k("vector", 64, 104)
-        cast_k("scalar", 104, 128)
-        cast_q("scalar", 0)
-        k_mx = quantize("k", k_bf[:].rearrange("p r s j -> p (r s j)"), N)
-        quant_q(0)
-        scores(0)
-        make_mt(0)
-        cast_q("vector", 1)
-        tanh(0)
-        quant_q(1)
-        scores(1)
+        def cast_v(engine):
+            cast(engine, v_bf[:].rearrange("p (c i r) -> p c r i", i=2, r=PACK),
+                 v_raw[:].rearrange("p r (c i) -> p c r i", i=2))
 
-        for u in range(UNITS):
-            k = u // 2
-            if u > 0:
-                tanh(u)
-            if u % 2 == 1 and k + 2 < PAIRS:
-                cast_q("scalar", k + 2)
-            if u == 2:
-                cast("scalar", v_bf[:].rearrange("p (c i r) -> p c r i", i=4, r=PACK),
-                     v_raw[:].rearrange("p r (c i) -> p c r i", i=4))
-            if u % H == 0 and u > 0:
-                sigmoid(u // H - 1)
-            if u == UNITS - 2:
-                sigmoid(CHUNKS - 1)
-            weigh(u)
-            if u % 2 == 0 and 2 <= k + 1 < PAIRS:
-                quant_q(k + 1)
-                scores(k + 1)
-            if u > 0:
-                quant_w(u - 1)
-            if u == 3:
-                v_mx.append(quantize("v", v_bf[:], E))
-                for uu in range(3):
-                    second(uu)
-            if u > 3:
-                second(u - 1)
-            if u % H == 3 and u + 1 < UNITS:
-                make_mt(u // H + 1)
-            if u % H == 1 and u > H:
-                finish(u // H - 1, 0, H)
-        finish(CHUNKS - 1, 0, 2)
-        quant_w(UNITS - 1)
-        second(UNITS - 1)
-        finish(CHUNKS - 1, 2, 3)
-        finish(CHUNKS - 1, 3, 4)
+        def quant_v():
+            v_mx.append(quantize("v", v_bf[:], E))
+
+        def quant_k():
+            k_mx.extend(quantize("k", k_bf[:].rearrange("p r s j -> p (r s j)"), N))
+
+        k_mx = []
+
+        def quant_and_score(k):
+            quant_q(k)
+            scores(k)
+
+        steps = {
+            "T": tanh, "C": cast_q, "QQ": quant_q, "S": scores, "M": make_mt, "W": weigh, "QW": quant_w,
+            "PV": second, "G": sigmoid, "F": finish, "CV": cast_v, "QV": quant_v, "CK": cast_k, "QK": quant_k,
+        }
+        for step in SCHEDULE:
+            steps[step[0]](*step[1:])

@@ -9,6 +9,7 @@ F32 = mybir.dt.float32
 BF16 = mybir.dt.bfloat16
 U32 = mybir.dt.uint32
 U8 = mybir.dt.uint8
+I32 = mybir.dt.int32
 FP8X4 = mybir.dt.float8_e4m3fn_x4
 ACT = mybir.ActivationFunctionType
 ALU = mybir.AluOpType
@@ -20,9 +21,12 @@ QC = 128
 CHUNKS = NQ // QC
 UNITS = CHUNKS * H
 PAIRS = UNITS // 2
-ORDER = [(0, 0), (0, 1), (1, 0), (1, 1), (2, 0), (2, 1), (3, 0), (3, 1)]
-LOADS = [("q", 0, 0, 1), ("q", 1, 0, 1), ("m", 0, 1), ("q", 0, 1, 2), ("q", 1, 1, 2), ("v",), ("m", 1, 2), ("q", 0, 2, 4), ("q", 1, 2, 4), ("og", 1), ("m", 2, 4), ("og", 0), ("og", 3), ("og", 2)]
-SCHEDULE = [("CK", "scalar", 104, 128), ("CK", "vector", 0, 64), ("CK", "vector", 64, 104), ("C", "scalar", 0), ("QK",), ("QQ", 0), ("S", 0), ("C", "scalar", 1), ("QQ", 1), ("M", 0), ("C", "vector", 2), ("S", 1), ("T", 0), ("T", 1), ("W", 0, 0, 1), ("QQ", 2), ("S", 2), ("W", 0, 1, 2), ("T", 2), ("C", "scalar", 3), ("T", 3), ("CV", "scalar"), ("QW", 0, 0, 2), ("QQ", 3), ("T", 4), ("S", 3), ("M", 1), ("W", 1, 0, 2), ("T", 5), ("QV",), ("QW", 1, 0, 2), ("C", "scalar", 6), ("W", 2, 0, 1), ("C", "scalar", 4), ("T", 6), ("T", 7), ("W", 2, 1, 2), ("QQ", 4), ("QQ", 6), ("W", 3, 0, 1), ("S", 4), ("PV", 0), ("PV", 3), ("C", "scalar", 5), ("W", 3, 1, 2), ("PV", 1), ("T", 8), ("G", 1), ("S", 6), ("PV", 2), ("T", 9), ("QW", 2, 0, 2), ("M", 2), ("M", 3), ("PV", 4), ("QQ", 5), ("T", 12), ("QW", 3, 0, 2), ("PV", 5), ("S", 5), ("PV", 7), ("W", 4, 0, 2), ("PV", 6), ("G", 0), ("T", 10), ("T", 11), ("F", 0, 0, 4), ("C", "scalar", 7), ("T", 13), ("QW", 4, 0, 2), ("W", 5, 0, 1), ("W", 5, 1, 2), ("QQ", 7), ("W", 6, 0, 2), ("S", 7), ("PV", 8), ("T", 14), ("PV", 9), ("QW", 5, 0, 2), ("G", 2), ("T", 15), ("QW", 6, 0, 2), ("F", 1, 0, 4), ("W", 7, 0, 1), ("PV", 11), ("PV", 10), ("F", 2, 0, 4), ("PV", 12), ("W", 7, 1, 2), ("QW", 7, 0, 1), ("PV", 13), ("PV", 14), ("QW", 7, 1, 2), ("G", 3), ("F", 3, 0, 2), ("PV", 15), ("F", 3, 2, 4)]
+MT_GROUPS = [(0, 1), (1, 2), (2, 4)]
+ORDER = [(0, 0, 2), (1, 0, 2), (0, 1, 3), (1, 1, 3), (2, 0, 1), (2, 2, 3), (3, 0, 1), (3, 2, 3)]
+SPLIT = 2
+EARLY = 5
+LOADS = [("q", 1, 0, 1), ("q", 0, 1, 2), ("q", 1, 1, 2), ("m", 0, 1), ("m", 1, 2), ("v",), ("q", 0, 2, 4), ("m", 2, 4), ("q", 1, 2, 4), ("og", 0), ("og", 1), ("og", 2), ("og", 3)]
+SCHEDULE = [("C", "scalar", 0), ("CK", "vector", 0, 64), ("CK", "scalar", 104, 128), ("QQ", 0), ("CK", "vector", 64, 104), ("QK", 0), ("QK", 1), ("QK", 2), ("QK", 3), ("C", "scalar", 1), ("S", 0, 0, 1), ("C", "vector", 2), ("QQ", 1), ("T", 0), ("QQ", 2), ("X",), ("C", "vector", 3), ("QQ", 3), ("M", "scalar", 0, 2), ("M", "vector", 0, 3), ("M", "vector", 0, 1), ("M", "vector", 0, 0), ("S", 0, 1, 2), ("T", 1), ("W", 0, 0, 1), ("S", 1, 0, 1), ("T", 2), ("W", 0, 1, 2), ("M", "vector", 1, 3), ("S", 1, 1, 2), ("S", 3, 0, 1), ("M", "vector", 1, 2), ("M", "scalar", 1, 1), ("S", 3, 1, 2), ("M", "scalar", 1, 0), ("T", 3), ("CV", "scalar"), ("QW", 0, 0, 2), ("W", 1, 0, 1), ("S", 2, 0, 1), ("W", 1, 1, 2), ("QV",), ("C", "vector", 4), ("T", 6), ("QW", 1, 0, 2), ("S", 2, 1, 2), ("PV", 0), ("QQ", 4), ("T", 7), ("W", 3, 0, 2), ("PV", 2), ("C", "scalar", 6), ("QQ", 6), ("PV", 3), ("S", 4, 0, 2), ("QW", 3, 0, 2), ("T", 4), ("T", 5), ("PV", 1), ("W", 2, 0, 2), ("M", "scalar", 2, 2), ("S", 6, 0, 2), ("C", "vector", 5), ("QW", 2, 0, 2), ("M", "scalar", 2, 3), ("PV", 4), ("M", "scalar", 2, 0), ("QQ", 5), ("M", "scalar", 2, 1), ("T", 8), ("T", 9), ("W", 4, 0, 1), ("W", 4, 1, 2), ("C", "scalar", 7), ("QQ", 7), ("QW", 4, 0, 2), ("PV", 6), ("T", 12), ("W", 6, 0, 1), ("T", 13), ("S", 5, 0, 2), ("W", 6, 1, 2), ("PV", 5), ("G", 0), ("F", 0, 0, 4), ("QW", 6, 0, 2), ("PV", 7), ("S", 7, 0, 2), ("T", 10), ("T", 11), ("W", 5, 0, 2), ("G", 1), ("F", 1, 0, 4), ("PV", 8), ("PV", 9), ("T", 14), ("QW", 5, 0, 2), ("T", 15), ("PV", 12), ("G", 2), ("W", 7, 0, 2), ("PV", 11), ("PV", 10), ("F", 2, 0, 4), ("QW", 7, 0, 1), ("QW", 7, 1, 2), ("G", 3), ("PV", 13), ("F", 3, 0, 2), ("PV", 14), ("PV", 15), ("F", 3, 2, 4)]
 
 
 def tile_rows_a_tanh_mask_gate_kernel(tc, qT, kT, t, v, mask, og, out):
@@ -44,28 +48,27 @@ def tile_rows_a_tanh_mask_gate_kernel(tc, qT, kT, t, v, mask, og, out):
         for a in range(2):
             cols = slice(a * (N // 2), (a + 1) * (N // 2))
             nc.sync.dma_start(out=k_raw[a][0:ROWS], in_=k_view[:, :, cols])
-            nc.scalar.dma_start(out=k_raw[a][ROWS:P], in_=k_view[:, :, cols])
-        t_sb = sb("t_sb", [P, PACK], F32)
-        nc.scalar.dma_start(out=t_sb[:], in_=t.rearrange("(p r) o -> p (r o)", r=PACK))
-        nc.scalar.activation(out=warm_out[:], in_=warm[:], func=ACT.Sigmoid)
+        k_mx = sb("k_mx", [P, N + N // 4], I32)
+        k_codes = k_mx[:, 0:N]
+        k_scales = k_mx[:, N : N + N // 4].bitcast(U8)
+        nc.vector.memset(k_mx[0:ROWS, N : N + N // 4], 0)
 
         q_view = qT.rearrange("(g h) (p j) q -> g (h p) j q", h=2, j=PACK)
         m_view = mask.rearrange("(p r) q -> p r q", r=PACK)
         q_raw = {}
-        m_raw = {}
+        m_group = {}
         og_raw = {}
 
-        def load_q(pair, c0, c1):
+        def load_q(pair, c0, c1, queue=nc.sync):
             tl = sb("q_raw%d_%d" % (pair, c0), [P, PACK, (c1 - c0) * QC], F32)
-            nc.sync.dma_start(out=tl[:], in_=q_view[pair][:, :, c0 * QC : c1 * QC])
+            queue.dma_start(out=tl[:], in_=q_view[pair][:, :, c0 * QC : c1 * QC])
             for c in range(c0, c1):
                 q_raw[(c, pair)] = tl[:, :, (c - c0) * QC : (c - c0 + 1) * QC]
 
         def load_m(c0, c1):
             tl = sb("m_raw%d" % c0, [P, PACK, (c1 - c0) * QC], F32)
             nc.sync.dma_start(out=tl[:], in_=m_view[:, :, c0 * QC : c1 * QC])
-            for c in range(c0, c1):
-                m_raw[c] = tl[:, :, (c - c0) * QC : (c - c0 + 1) * QC]
+            m_group[c0] = tl
 
         def load_og(c):
             tl = sb("og_raw%d" % c, [P, H, E], F32)
@@ -78,7 +81,11 @@ def tile_rows_a_tanh_mask_gate_kernel(tc, qT, kT, t, v, mask, og, out):
             nc.sync.dma_start(out=v_raw[:], in_=v[0].rearrange("(p r) e -> p r e", r=PACK))
 
         loads = {"q": load_q, "m": load_m, "og": load_og, "v": load_v}
-        for step in LOADS:
+        load_q(0, 0, 1, nc.scalar)
+        t_sb = sb("t_sb", [P, PACK], F32)
+        nc.scalar.dma_start(out=t_sb[:], in_=t.rearrange("(p r) o -> p (r o)", r=PACK))
+        nc.scalar.activation(out=warm_out[:], in_=warm[:], func=ACT.Sigmoid)
+        for step in LOADS[:EARLY]:
             loads[step[0]](*step[1:])
 
         def cast(engine, out_ap, in_ap):
@@ -97,16 +104,16 @@ def tile_rows_a_tanh_mask_gate_kernel(tc, qT, kT, t, v, mask, og, out):
 
         def cast_k(engine, s0, s1):
             a = s0 // ROWS
-            src = k_raw[a][:, :, (s0 - a * ROWS) * PACK : (s1 - a * ROWS) * PACK]
-            cast(engine, k_bf[:, :, s0:s1, :].rearrange("p (a b) s j -> p a s j b", b=2),
+            src = k_raw[a][0:ROWS, :, (s0 - a * ROWS) * PACK : (s1 - a * ROWS) * PACK]
+            cast(engine, k_bf[0:ROWS, :, s0:s1, :].rearrange("p (a b) s j -> p a s j b", b=2),
                  src.rearrange("p j (s a b) -> p a s j b", a=2, b=2))
 
         q_bf = {}
         q_mx = {}
 
         def cast_q(engine, k):
-            c, pair = ORDER[k]
-            tl = sb("q_bf%d" % k, [P, QC * PACK], BF16, tag="q_bf", bufs=4)
+            c, pair = divmod(k, 2)
+            tl = sb("q_bf%d" % k, [P, QC * PACK], BF16, tag="q_bf", bufs=8)
             cast(engine, tl[:].rearrange("p (c i j) -> p c j i", i=2, j=PACK),
                  q_raw[(c, pair)].rearrange("p j (c i) -> p c j i", i=2))
             q_bf[k] = tl
@@ -115,32 +122,37 @@ def tile_rows_a_tanh_mask_gate_kernel(tc, qT, kT, t, v, mask, og, out):
             q_mx[k] = quantize("q%d" % k, q_bf[k][:], QC)
 
         mt = {}
+        mt_group = {}
 
-        def make_mt(c):
-            tl = sb("mt%d" % c, [P, QC * PACK], F32)
-            nc.vector.tensor_tensor(
-                out=tl[:].rearrange("p (c i r) -> p c r i", i=2, r=PACK),
-                in0=m_raw[c].rearrange("p r (c i) -> p c r i", i=2),
-                in1=t_sb[:].unsqueeze(1).unsqueeze(3).to_broadcast([P, QC // 2, PACK, 2]),
-                op=ALU.mult)
-            mt[c] = tl
+        for c0, c1 in MT_GROUPS:
+            group = sb("mt%d" % c0, [P, (c1 - c0) * QC // 4, PACK, 4], F32)
+            mt_group[c0] = group
+            for c in range(c0, c1):
+                mt[c] = group[:, (c - c0) * QC // 4 : (c - c0 + 1) * QC // 4].rearrange("p c r i -> p (c r i)")
+
+        def make_mt(engine, c0, r):
+            dst = mt_group[c0][:, :, r, :]
+            src = m_group[c0][:, r, :].rearrange("p (c i) -> p c i", i=4)
+            if engine == "vector":
+                nc.vector.tensor_scalar(out=dst, in0=src, scalar1=t_sb[:, r : r + 1], scalar2=None, op0=ALU.mult)
+            else:
+                nc.scalar.activation(out=dst, in_=src, func=ACT.Copy, scale=t_sb[:, r : r + 1])
 
         score = {}
 
-        def scores(k):
-            banks = []
-            for g in range(2):
-                bank = psum.tile([P, PACK, QC], F32, name="score%d_%d" % (k, g), tag="score%d" % g, bufs=3)
-                banks.append(bank)
-                score[2 * k + g] = bank
-            q_codes, q_scales = q_mx[k]
-            for g in range(2):
-                rows = slice(g * ROWS, (g + 1) * ROWS)
-                for r in range(PACK):
-                    cols = slice(r * P, (r + 1) * P)
+        def scores(k, g0, g1):
+            c, heads = ORDER[k][0], ORDER[k][1:]
+            for g in range(g0, g1):
+                score[2 * k + g] = psum.tile(
+                    [P, PACK, QC], F32, name="score%d_%d" % (k, g), tag="score%d" % (heads[g] % 2), bufs=3)
+            for r in range(PACK):
+                cols = slice(r * P, (r + 1) * P)
+                for g in range(g0, g1):
+                    rows = slice(heads[g] % 2 * ROWS, (heads[g] % 2 + 1) * ROWS)
+                    q_codes, q_scales = q_mx[2 * c + heads[g] // 2]
                     nc.tensor.matmul_mx(
-                        out=banks[g][:, r, :],
-                        lhsT=k_mx[0][rows, cols].bitcast(FP8X4), lhsT_scale=k_mx[1][rows, cols],
+                        out=score[2 * k + g][:, r, :],
+                        lhsT=k_codes[rows, cols].bitcast(FP8X4), lhsT_scale=k_scales[rows, cols],
                         rhs=q_codes[rows, :].bitcast(FP8X4), rhs_scale=q_scales[rows, :],
                         start=True, stop=True)
 
@@ -149,20 +161,23 @@ def tile_rows_a_tanh_mask_gate_kernel(tc, qT, kT, t, v, mask, og, out):
         def tanh(u):
             k, g = divmod(u, 2)
             if g == 0:
-                pt[k] = sb("p%d" % k, [P, 2, QC * PACK], F32, tag="p", bufs=4)
+                pt[k] = sb("p%d" % k, [P, 2, QC * PACK], F32, tag="p", bufs=8)
             nc.scalar.activation(
-                out=pt[k][:, g, :].rearrange("p (q r) -> p q r", r=PACK),
-                in_=score[u][:].rearrange("p r q -> p q r"), func=ACT.Tanh)
+                out=pt[k][:, g, :].rearrange("p (c r i) -> p c r i", r=PACK, i=4),
+                in_=score[u][:].rearrange("p r (c i) -> p c r i", i=4), func=ACT.Tanh)
 
         w_bf = {}
         w_mx = {}
 
         def weigh(k, g0, g1):
             if g0 == 0:
-                w_bf[k] = sb("w_bf%d" % k, [P, 2, QC * PACK], BF16, tag="w_bf", bufs=4)
+                w_bf[k] = sb("w_bf%d" % k, [P, 2, QC * PACK], BF16, tag="w_bf", bufs=8)
             nc.vector.tensor_tensor(
-                out=w_bf[k][:, g0:g1, :], in0=pt[k][:, g0:g1, :],
-                in1=mt[ORDER[k][0]][:].unsqueeze(1).to_broadcast([P, g1 - g0, QC * PACK]), op=ALU.mult)
+                out=w_bf[k][:, g0:g1, :].rearrange("p g (c i r) -> p g c r i", i=4, r=PACK),
+                in0=pt[k][:, g0:g1, :].rearrange("p g (c r i) -> p g c r i", i=4, r=PACK),
+                in1=mt[ORDER[k][0]].unsqueeze(1).to_broadcast([P, g1 - g0, QC * PACK])
+                .rearrange("p g (c r i) -> p g c r i", i=4, r=PACK),
+                op=ALU.mult)
 
         def quant_w(k, g0, g1):
             codes, scales = quantize("w%d_%d" % (k, g0), w_bf[k][:, g0:g1, :].rearrange("p g x -> p (g x)"), (g1 - g0) * QC)
@@ -173,10 +188,10 @@ def tile_rows_a_tanh_mask_gate_kernel(tc, qT, kT, t, v, mask, og, out):
         y = {}
 
         def second(u):
-            c, h = ORDER[u // 2][0], 2 * ORDER[u // 2][1] + u % 2
-            if h == 0 or u == UNITS - 2:
+            c, h = ORDER[u // 2][0], ORDER[u // 2][1 + u % 2]
+            if h == 0 or (c, h) == (CHUNKS - 1, SPLIT):
                 bank = psum.tile([P, H, E], F32, name="y%d" % u, tag="y", bufs=2)
-                for hh in range(h, H):
+                for hh in range(h, H if c < CHUNKS - 1 or h > 0 else SPLIT):
                     y[(c, hh)] = bank
             nc.tensor.matmul_mx(
                 out=y[(c, h)][:, h, :],
@@ -209,18 +224,20 @@ def tile_rows_a_tanh_mask_gate_kernel(tc, qT, kT, t, v, mask, og, out):
         def quant_v():
             v_mx.append(quantize("v", v_bf[:], E))
 
-        def quant_k():
-            k_mx.extend(quantize("k", k_bf[:].rearrange("p r s j -> p (r s j)"), N))
+        def quant_k(r):
+            cols = slice(r * P, (r + 1) * P)
+            nc.vector.quantize_mx(
+                out=k_codes[0:ROWS, cols].bitcast(FP8X4), scales=k_scales[0:ROWS, cols],
+                in_=k_bf[0:ROWS, r].rearrange("p s j -> p (s j)"))
 
-        k_mx = []
-
-        def quant_and_score(k):
-            quant_q(k)
-            scores(k)
+        def spread_k():
+            nc.sync.dma_start(out=k_mx[ROWS:P], in_=k_mx[0:ROWS])
+            for step in LOADS[EARLY:]:
+                loads[step[0]](*step[1:])
 
         steps = {
             "T": tanh, "C": cast_q, "QQ": quant_q, "S": scores, "M": make_mt, "W": weigh, "QW": quant_w,
-            "PV": second, "G": sigmoid, "F": finish, "CV": cast_v, "QV": quant_v, "CK": cast_k, "QK": quant_k,
+            "PV": second, "G": sigmoid, "F": finish, "CV": cast_v, "QV": quant_v, "CK": cast_k, "QK": quant_k, "X": spread_k,
         }
         for step in SCHEDULE:
             steps[step[0]](*step[1:])

from contextlib import ExitStack

import concourse.mybir as mybir

H, D, NQ, N, E = 4, 256, 512, 512, 128
FLOPS = 2 * H * NQ * N * (D + E)

F32 = mybir.dt.float32
BF16 = mybir.dt.bfloat16
U32 = mybir.dt.uint32
U8 = mybir.dt.uint8
I32 = mybir.dt.int32
FP8X4 = mybir.dt.float8_e4m3fn_x4
ACT = mybir.ActivationFunctionType
ALU = mybir.AluOpType

P = 128
PACK = 4
ROWS = 64
QC = 128
CHUNKS = NQ // QC
UNITS = CHUNKS * H
PAIRS = UNITS // 2
MT_GROUPS = [(0, 1), (1, 2), (2, 4)]
ORDER = [(0, 0, 2), (1, 0, 2), (0, 1, 3), (1, 1, 3), (2, 0, 1), (2, 2, 3), (3, 0, 1), (3, 2, 3)]
SPLIT = 2
EARLY = 5
LOADS = [("q", 1, 0, 1), ("q", 0, 1, 2), ("q", 1, 1, 2), ("m", 0, 1), ("m", 1, 2), ("v",), ("q", 0, 2, 4), ("m", 2, 4), ("q", 1, 2, 4), ("og", 0), ("og", 1), ("og", 2), ("og", 3)]
SCHEDULE = [("C", "scalar", 0), ("CK", "vector", 0, 64), ("CK", "scalar", 104, 128), ("QQ", 0), ("CK", "vector", 64, 104), ("QK", 0), ("QK", 1), ("QK", 2), ("QK", 3), ("C", "scalar", 1), ("S", 0, 0, 1), ("C", "vector", 2), ("QQ", 1), ("T", 0), ("QQ", 2), ("X",), ("C", "vector", 3), ("QQ", 3), ("M", "scalar", 0, 2), ("M", "vector", 0, 3), ("M", "vector", 0, 1), ("M", "vector", 0, 0), ("S", 0, 1, 2), ("T", 1), ("W", 0, 0, 1), ("S", 1, 0, 1), ("T", 2), ("W", 0, 1, 2), ("M", "vector", 1, 3), ("S", 1, 1, 2), ("S", 3, 0, 1), ("M", "vector", 1, 2), ("M", "scalar", 1, 1), ("S", 3, 1, 2), ("M", "scalar", 1, 0), ("T", 3), ("CV", "scalar"), ("QW", 0, 0, 2), ("W", 1, 0, 1), ("S", 2, 0, 1), ("W", 1, 1, 2), ("QV",), ("C", "vector", 4), ("T", 6), ("QW", 1, 0, 2), ("S", 2, 1, 2), ("PV", 0), ("QQ", 4), ("T", 7), ("W", 3, 0, 2), ("PV", 2), ("C", "scalar", 6), ("QQ", 6), ("PV", 3), ("S", 4, 0, 2), ("QW", 3, 0, 2), ("T", 4), ("T", 5), ("PV", 1), ("W", 2, 0, 2), ("M", "scalar", 2, 2), ("S", 6, 0, 2), ("C", "vector", 5), ("QW", 2, 0, 2), ("M", "scalar", 2, 3), ("PV", 4), ("M", "scalar", 2, 0), ("QQ", 5), ("M", "scalar", 2, 1), ("T", 8), ("T", 9), ("W", 4, 0, 1), ("W", 4, 1, 2), ("C", "scalar", 7), ("QQ", 7), ("QW", 4, 0, 2), ("PV", 6), ("T", 12), ("W", 6, 0, 1), ("T", 13), ("S", 5, 0, 2), ("W", 6, 1, 2), ("PV", 5), ("G", 0), ("F", 0, 0, 4), ("QW", 6, 0, 2), ("PV", 7), ("S", 7, 0, 2), ("T", 10), ("T", 11), ("W", 5, 0, 2), ("G", 1), ("F", 1, 0, 4), ("PV", 8), ("PV", 9), ("T", 14), ("QW", 5, 0, 2), ("T", 15), ("PV", 12), ("G", 2), ("W", 7, 0, 2), ("PV", 11), ("PV", 10), ("F", 2, 0, 4), ("QW", 7, 0, 1), ("QW", 7, 1, 2), ("G", 3), ("PV", 13), ("F", 3, 0, 2), ("PV", 14), ("PV", 15), ("F", 3, 2, 4)]


def tile_rows_a_tanh_mask_gate_kernel(tc, qT, kT, t, v, mask, og, out):
    nc = tc.nc
    with ExitStack() as ctx:
        keep = ctx.enter_context(tc.tile_pool(name="keep", bufs=1))
        psum = ctx.enter_context(tc.psum_pool(name="psum", bufs=1))
        ctx.enter_context(tc.manual_schedule())

        def sb(name, shape, dtype, tag=None, bufs=1):
            return keep.tile(shape, dtype, name=name, tag=tag or name, bufs=bufs, align_bytes=64)

        warm = sb("warm", [P, 8], F32)
        nc.vector.memset(warm[:], 0.0)
        warm_out = sb("warm_out", [P, 8], F32)

        k_view = kT[0].rearrange("(p j) n -> p j n", j=PACK)
        k_raw = [sb("k_raw%d" % a, [P, PACK, N // 2], F32) for a in range(2)]
        for a in range(2):
            cols = slice(a * (N // 2), (a + 1) * (N // 2))
            nc.sync.dma_start(out=k_raw[a][0:ROWS], in_=k_view[:, :, cols])
        k_mx = sb("k_mx", [P, N + N // 4], I32)
        k_codes = k_mx[:, 0:N]
        k_scales = k_mx[:, N : N + N // 4].bitcast(U8)
        nc.vector.memset(k_mx[0:ROWS, N : N + N // 4], 0)

        q_view = qT.rearrange("(g h) (p j) q -> g (h p) j q", h=2, j=PACK)
        m_view = mask.rearrange("(p r) q -> p r q", r=PACK)
        q_raw = {}
        m_group = {}
        og_raw = {}

        def load_q(pair, c0, c1, queue=nc.sync):
            tl = sb("q_raw%d_%d" % (pair, c0), [P, PACK, (c1 - c0) * QC], F32)
            queue.dma_start(out=tl[:], in_=q_view[pair][:, :, c0 * QC : c1 * QC])
            for c in range(c0, c1):
                q_raw[(c, pair)] = tl[:, :, (c - c0) * QC : (c - c0 + 1) * QC]

        def load_m(c0, c1):
            tl = sb("m_raw%d" % c0, [P, PACK, (c1 - c0) * QC], F32)
            nc.sync.dma_start(out=tl[:], in_=m_view[:, :, c0 * QC : c1 * QC])
            m_group[c0] = tl

        def load_og(c):
            tl = sb("og_raw%d" % c, [P, H, E], F32)
            nc.sync.dma_start(out=tl[:], in_=og[:, c * QC : (c + 1) * QC, :].rearrange("h q e -> q h e"))
            og_raw[c] = tl

        v_raw = sb("v_raw", [P, PACK, E], F32)

        def load_v():
            nc.sync.dma_start(out=v_raw[:], in_=v[0].rearrange("(p r) e -> p r e", r=PACK))

        loads = {"q": load_q, "m": load_m, "og": load_og, "v": load_v}
        load_q(0, 0, 1, nc.scalar)
        t_sb = sb("t_sb", [P, PACK], F32)
        nc.scalar.dma_start(out=t_sb[:], in_=t.rearrange("(p r) o -> p (r o)", r=PACK))
        nc.scalar.activation(out=warm_out[:], in_=warm[:], func=ACT.Sigmoid)
        for step in LOADS[:EARLY]:
            loads[step[0]](*step[1:])

        def cast(engine, out_ap, in_ap):
            if engine == "vector":
                nc.vector.tensor_copy(out=out_ap, in_=in_ap)
            else:
                nc.scalar.copy(out=out_ap, in_=in_ap)

        def quantize(name, grouped, width):
            codes = sb(name + "_codes", [P, width], U32)
            scales = sb(name + "_scales", [P, width], U8)
            nc.vector.quantize_mx(out=codes[:].bitcast(FP8X4), scales=scales[:], in_=grouped)
            return codes, scales

        k_bf = sb("k_bf", [P, PACK, P, PACK], BF16)

        def cast_k(engine, s0, s1):
            a = s0 // ROWS
            src = k_raw[a][0:ROWS, :, (s0 - a * ROWS) * PACK : (s1 - a * ROWS) * PACK]
            cast(engine, k_bf[0:ROWS, :, s0:s1, :].rearrange("p (a b) s j -> p a s j b", b=2),
                 src.rearrange("p j (s a b) -> p a s j b", a=2, b=2))

        q_bf = {}
        q_mx = {}

        def cast_q(engine, k):
            c, pair = divmod(k, 2)
            tl = sb("q_bf%d" % k, [P, QC * PACK], BF16, tag="q_bf", bufs=8)
            cast(engine, tl[:].rearrange("p (c i j) -> p c j i", i=2, j=PACK),
                 q_raw[(c, pair)].rearrange("p j (c i) -> p c j i", i=2))
            q_bf[k] = tl

        def quant_q(k):
            q_mx[k] = quantize("q%d" % k, q_bf[k][:], QC)

        mt = {}
        mt_group = {}

        for c0, c1 in MT_GROUPS:
            group = sb("mt%d" % c0, [P, (c1 - c0) * QC // 4, PACK, 4], F32)
            mt_group[c0] = group
            for c in range(c0, c1):
                mt[c] = group[:, (c - c0) * QC // 4 : (c - c0 + 1) * QC // 4].rearrange("p c r i -> p (c r i)")

        def make_mt(engine, c0, r):
            dst = mt_group[c0][:, :, r, :]
            src = m_group[c0][:, r, :].rearrange("p (c i) -> p c i", i=4)
            if engine == "vector":
                nc.vector.tensor_scalar(out=dst, in0=src, scalar1=t_sb[:, r : r + 1], scalar2=None, op0=ALU.mult)
            else:
                nc.scalar.activation(out=dst, in_=src, func=ACT.Copy, scale=t_sb[:, r : r + 1])

        score = {}

        def scores(k, g0, g1):
            c, heads = ORDER[k][0], ORDER[k][1:]
            for g in range(g0, g1):
                score[2 * k + g] = psum.tile(
                    [P, PACK, QC], F32, name="score%d_%d" % (k, g), tag="score%d" % (heads[g] % 2), bufs=3)
            for r in range(PACK):
                cols = slice(r * P, (r + 1) * P)
                for g in range(g0, g1):
                    rows = slice(heads[g] % 2 * ROWS, (heads[g] % 2 + 1) * ROWS)
                    q_codes, q_scales = q_mx[2 * c + heads[g] // 2]
                    nc.tensor.matmul_mx(
                        out=score[2 * k + g][:, r, :],
                        lhsT=k_codes[rows, cols].bitcast(FP8X4), lhsT_scale=k_scales[rows, cols],
                        rhs=q_codes[rows, :].bitcast(FP8X4), rhs_scale=q_scales[rows, :],
                        start=True, stop=True)

        pt = {}

        def tanh(u):
            k, g = divmod(u, 2)
            if g == 0:
                pt[k] = sb("p%d" % k, [P, 2, QC * PACK], F32, tag="p", bufs=8)
            nc.scalar.activation(
                out=pt[k][:, g, :].rearrange("p (c r i) -> p c r i", r=PACK, i=4),
                in_=score[u][:].rearrange("p r (c i) -> p c r i", i=4), func=ACT.Tanh)

        w_bf = {}
        w_mx = {}

        def weigh(k, g0, g1):
            if g0 == 0:
                w_bf[k] = sb("w_bf%d" % k, [P, 2, QC * PACK], BF16, tag="w_bf", bufs=8)
            nc.vector.tensor_tensor(
                out=w_bf[k][:, g0:g1, :].rearrange("p g (c i r) -> p g c r i", i=4, r=PACK),
                in0=pt[k][:, g0:g1, :].rearrange("p g (c r i) -> p g c r i", i=4, r=PACK),
                in1=mt[ORDER[k][0]].unsqueeze(1).to_broadcast([P, g1 - g0, QC * PACK])
                .rearrange("p g (c r i) -> p g c r i", i=4, r=PACK),
                op=ALU.mult)

        def quant_w(k, g0, g1):
            codes, scales = quantize("w%d_%d" % (k, g0), w_bf[k][:, g0:g1, :].rearrange("p g x -> p (g x)"), (g1 - g0) * QC)
            for g in range(g0, g1):
                cols = slice((g - g0) * QC, (g - g0 + 1) * QC)
                w_mx[2 * k + g] = (codes[:, cols], scales[:, cols])

        y = {}

        def second(u):
            c, h = ORDER[u // 2][0], ORDER[u // 2][1 + u % 2]
            if h == 0 or (c, h) == (CHUNKS - 1, SPLIT):
                bank = psum.tile([P, H, E], F32, name="y%d" % u, tag="y", bufs=2)
                for hh in range(h, H if c < CHUNKS - 1 or h > 0 else SPLIT):
                    y[(c, hh)] = bank
            nc.tensor.matmul_mx(
                out=y[(c, h)][:, h, :],
                lhsT=w_mx[u][0].bitcast(FP8X4), lhsT_scale=w_mx[u][1],
                rhs=v_mx[0][0][:].bitcast(FP8X4), rhs_scale=v_mx[0][1][:],
                start=True, stop=True)

        gate = {}

        def sigmoid(c):
            tl = sb("gate%d" % c, [P, H, E], F32)
            nc.scalar.activation(out=tl[:], in_=og_raw[c][:], func=ACT.Sigmoid)
            gate[c] = tl

        def finish(c, h0, h1):
            tl = sb("res%d_%d" % (c, h0), [P, h1 - h0, E], F32)
            nc.vector.scalar_tensor_tensor(
                out=tl[:], in0=y[(c, h0)][:, h0:h1, :], scalar=1.0 / 16.0, in1=gate[c][:, h0:h1, :],
                op0=ALU.mult, op1=ALU.mult)
            nc.sync.dma_start(
                out=out[h0:h1, c * QC : (c + 1) * QC, :].rearrange("h q e -> q h e"), in_=tl[:])

        v_bf = sb("v_bf", [P, E * PACK], BF16)
        v_mx = []

        def cast_v(engine):
            cast(engine, v_bf[:].rearrange("p (c i r) -> p c r i", i=2, r=PACK),
                 v_raw[:].rearrange("p r (c i) -> p c r i", i=2))

        def quant_v():
            v_mx.append(quantize("v", v_bf[:], E))

        def quant_k(r):
            cols = slice(r * P, (r + 1) * P)
            nc.vector.quantize_mx(
                out=k_codes[0:ROWS, cols].bitcast(FP8X4), scales=k_scales[0:ROWS, cols],
                in_=k_bf[0:ROWS, r].rearrange("p s j -> p (s j)"))

        def spread_k():
            nc.sync.dma_start(out=k_mx[ROWS:P], in_=k_mx[0:ROWS])
            for step in LOADS[EARLY:]:
                loads[step[0]](*step[1:])

        steps = {
            "T": tanh, "C": cast_q, "QQ": quant_q, "S": scores, "M": make_mt, "W": weigh, "QW": quant_w,
            "PV": second, "G": sigmoid, "F": finish, "CV": cast_v, "QV": quant_v, "CK": cast_k, "QK": quant_k, "X": spread_k,
        }
        for step in SCHEDULE:
            steps[step[0]](*step[1:])
